import numpy as np, ml_dtypes
CORES = [19,147,275,403]
N = 4
import mx_ref
NC, G = 192, 2
C = np.float32(0.043)
WID = [160,128,192,160]
BF = ml_dtypes.bfloat16
def cut(t, i, w=512):
    return t[:, w * i:w * i + w]
def tile(rs):
    return np.stack(rs, axis=2).reshape(128, -1).astype(BF)
def layer(w, X):
    out = []
    for i in range(G):
        for t in range(len(X)):
            p = mx_ref.matmul(mx_ref.quantize(cut(w, len(X) * i + t)), X[t])
            z = p if t == 0 else z + p
        out.append(z)
    return out
def act(Z):
    return [np.maximum(s * z, 0) * C for z in Z for s in (1, -1)]
def setup_inputs(rng):
    def f(*shape):
        return mx_ref.flush((rng.standard_normal(shape, dtype=np.float32) * np.exp2(rng.integers(-2, 3, shape[:-1] + (1,)))).astype(BF))
    return {"x": f(N, 128, 4 * NC), "w1": f(N, 128, G * 512), "w2": f(N, 128, 512)}
def setup_inputs_blocks(rng):
    d = setup_inputs(rng)
    for k in ("x", "w1", "w2"): d[k] = mx_ref.spread(d[k], rng, 2)
    return d
def setup_inputs_wide(rng):
    d = setup_inputs(rng)
    for k in ("x", "w1", "w2"): d[k] = mx_ref.flush((d[k].astype(np.float32) * np.exp2(rng.integers(-6, 7, (N, 1, 1))).astype(np.float32)).astype(BF))
    return d
def reference(x, w1, w2):
    X = [mx_ref.quantize(x[j][:, :4 * WID[j]]) for j in range(N)]
    y = np.full((N, 128, NC), np.nan, np.float32)
    for c in range(N):
        for r in range(N):
            p = mx_ref.matmul(mx_ref.quantize(w2[r]), mx_ref.quantize(tile(act(layer(w1[r], [X[c]])))))
            z = p if r == 0 else z + p
        y[c][:, :WID[c]] = z
    return {"y": y}

@@ -1,0 +1,140 @@
+from concourse.bass import DstId, RemoteDMATransfer
+from concourse.mybir import dt, AluOpType, ActivationFunctionType
+
+NMAX = 192
+PAIRS = ("a", "b", "c", "d")
+
+SCRATCH = {
+    "xin": ("sbuf", [128, 4 * NMAX], "bfloat16"),
+    "win": ("sbuf", [128, 1536], "bfloat16"),
+    "xq": ("sbuf", [128, NMAX], "float8_e4m3fn_x4"), "xs": ("sbuf", [128, NMAX], "uint8"),
+    "pq": ("sbuf", [128, NMAX], "float8_e4m3fn_x4"), "ps": ("sbuf", [128, NMAX], "uint8"),
+    "wq": ("sbuf", [128, 384], "float8_e4m3fn_x4"), "ws": ("sbuf", [128, 384], "uint8"),
+    "kq": ("sbuf", [128, 384], "float8_e4m3fn_x4"), "ks": ("sbuf", [128, 384], "uint8"),
+    "yout": ("sbuf", [128, NMAX], "float32"),
+    "yland": ("sbuf", [128, NMAX], "float32"),
+    "ysum": ("sbuf", [128, NMAX], "float32"),
+}
+for _n in range(6):
+    SCRATCH["z%d" % _n] = ("psum", [128, 512], "float32")
+for _n in ("ym", "yp"):
+    SCRATCH[_n] = ("psum", [128, 512], "float32")
+for _n in PAIRS:
+    SCRATCH["h" + _n] = ("sbuf", [128, 4 * NMAX], "bfloat16")
+    SCRATCH["hq" + _n] = ("sbuf", [128, NMAX], "float8_e4m3fn_x4")
+    SCRATCH["hs" + _n] = ("sbuf", [128, NMAX], "uint8")
+
+SEMAPHORES = ["lx", "lw1", "lw2", "qx", "qw1", "qw2", "sent", "gotx", "gotw1", "gotw2", "goty",
+              "ypdone", "ymdone", "ycopied", "ysummed", "stored"]
+for _n in PAIRS:
+    SEMAPHORES += ["z0" + _n, "z1" + _n, "h" + _n, "hq" + _n]
+
+
+def rank_program(g, core, T, topo):
+    rank = T.rank_of(core)
+    if rank is None:
+        return
+    S = T.sem
+    wid = T.tables["WID"]
+    scale = 0.043
+    rack = topo.rack(topo.host(core))
+    others = [c for c in T.cores if c != core]
+    mate = [c for c in others if topo.rack(topo.host(c)) == rack][0]
+    partner = [c for c in others if topo.rack(topo.host(c)) != rack and topo.may_write(core, c)][0]
+    n_m, n_p = wid[rank], wid[T.rank_of(partner)]
+    u8 = dt.uint8
+    n_sent = [0]
+    engines = {c: bin(topo.mask(core, c)).count("1") for c in (mate, partner)}
+
+    def send(dst, out, in_, sem):
+        rid, pid = topo.addr(dst, core)
+        g.remote_dma(out, in_, sem, S.sent, pid, rid, topo.mask(core, dst))
+        n_sent[0] += engines[dst]
+
+    g.sync.dma_start(T.xin[:, 0:4 * n_m], T.x[:, 0:4 * n_m]).then_inc(S.lx, 16)
+    g.sync.dma_start(T.win[:, 0:1024], T.w1[:, :]).then_inc(S.lw1, 16)
+    g.sync.dma_start(T.win[:, 1024:1536], T.w2[:, :]).then_inc(S.lw2, 16)
+
+    g.vector.wait_ge(S.lx, 16)
+    g.vector.quantize_mx(T.xq[:, 0:n_m], T.xs[:, 0:n_m], T.xin[:, 0:4 * n_m]).then_inc(S.qx, 1)
+    g.vector.wait_ge(S.lw1, 16)
+    g.vector.quantize_mx(T.wq[:, 0:256], T.ws[:, 0:256], T.win[:, 0:1024]).then_inc(S.qw1, 1)
+    g.vector.wait_ge(S.lw2, 16)
+    g.vector.quantize_mx(T.wq[:, 256:384], T.ws[:, 256:384], T.win[:, 1024:1536]).then_inc(S.qw2, 1)
+
+    g.wait_ge(S.qx, 1)
+    send(partner, T.pq[:, 0:n_m].bitcast(u8), T.xq[:, 0:n_m].bitcast(u8), S.gotx)
+    send(partner, T.ps[:, 0:n_m], T.xs[:, 0:n_m], S.gotx)
+    g.wait_ge(S.qw1, 1)
+    send(mate, T.kq[:, 0:256].bitcast(u8), T.wq[:, 0:256].bitcast(u8), S.gotw1)
+    g.wait_ge(S.qw2, 1)
+    send(mate, T.ks[:, :], T.ws[:, :], S.gotw1)
+    send(mate, T.kq[:, 256:384].bitcast(u8), T.wq[:, 256:384].bitcast(u8), S.gotw2)
+    g.wait_ge(S.ycopied, 1)
+    send(partner, T.yland[:, 0:n_p], T.yout[:, 0:n_p], S.goty)
+
+    own_w, mate_w = (T.wq, T.ws), (T.kq, T.ks)
+    own_x, part_x = (T.xq, T.xs, n_m), (T.pq, T.ps, n_p)
+    z_bank = {"a": (T.z0, T.z1), "b": (T.z2, T.z3), "c": (T.z4, T.z5), "d": (T.z0, T.z1)}
+
+    def first(p, w, x):
+        q, s, n = x
+        for i in range(2):
+            g.tensor.matmul_mx(z_bank[p][i][:, 0:n], w[0][:, 128 * i:128 * i + 128], w[1][:, 128 * i:128 * i + 128],
+                               q[:, 0:n], s[:, 0:n], True, True).then_inc(S["z%d%s" % (i, p)], 1)
+
+    def act_scalar(p, n):
+        h = T["h" + p]
+        g.scalar.wait_ge(S["z0" + p], 1)
+        for b, c in ((0, scale), (1, -scale)):
+            g.scalar.activation(h[:, b:4 * n:4], z_bank[p][0][:, 0:n], ActivationFunctionType.Relu, scale=c).then_inc(S["h" + p], 1)
+
+    def act_vector(p, n):
+        h = T["h" + p]
+        g.vector.wait_ge(S["z1" + p], 1)
+        for b, c in ((2, scale), (3, -scale)):
+            g.vector.tensor_scalar(h[:, b:4 * n:4], z_bank[p][1][:, 0:n], c, 0.0, AluOpType.mult, AluOpType.max).then_inc(S["h" + p], 1)
+        g.vector.wait_ge(S["h" + p], 4)
+        g.vector.quantize_mx(T["hq" + p][:, 0:n], T["hs" + p][:, 0:n], h[:, 0:4 * n]).then_inc(S["hq" + p], 1)
+
+    def second(p, w, y, n, start, done=None):
+        g.tensor.wait_ge(S["hq" + p], 1)
+        r = g.tensor.matmul_mx(y[:, 0:n], w[0][:, 256:384], w[1][:, 256:384], T["hq" + p][:, 0:n], T["hs" + p][:, 0:n], start, not start)
+        if done is not None:
+            r.then_inc(done, 1)
+
+    g.tensor.wait_ge(S.qx, 1)
+    g.tensor.wait_ge(S.qw1, 1)
+    first("a", own_w, own_x)
+    g.tensor.wait_ge(S.qw2, 1)
+    second("a", own_w, T.ym, n_m, True)
+    g.tensor.wait_ge(S.gotx, 2 * engines[partner])
+    first("b", own_w, part_x)
+    second("b", own_w, T.yp, n_p, True)
+    g.tensor.wait_ge(S.gotw1, 2 * engines[mate])
+    first("c", mate_w, part_x)
+    first("d", mate_w, own_x)
+    g.tensor.wait_ge(S.gotw2, engines[mate])
+    second("c", mate_w, T.yp, n_p, False, S.ypdone)
+    second("d", mate_w, T.ym, n_m, False, S.ymdone)
+
+    act_scalar("a", n_m)
+    act_scalar("b", n_p)
+    act_scalar("c", n_p)
+    g.scalar.wait_ge(S.ypdone, 1)
+    g.scalar.activation(T.yout[:, 0:n_p], T.yp[:, 0:n_p], ActivationFunctionType.Copy).then_inc(S.ycopied, 1)
+    act_scalar("d", n_m)
+
+    act_vector("a", n_m)
+    act_vector("b", n_p)
+    act_vector("c", n_p)
+    act_vector("d", n_m)
+    g.vector.wait_ge(S.ymdone, 1)
+    g.vector.wait_ge(S.goty, engines[partner])
+    g.vector.tensor_tensor(T.ysum[:, 0:n_m], T.ym[:, 0:n_m], T.yland[:, 0:n_m], AluOpType.add).then_inc(S.ysummed, 1)
+
+    g.sync.wait_ge(S.ysummed, 1)
+    g.sync.dma_start(T.y[:, 0:n_m], T.ysum[:, 0:n_m]).then_inc(S.stored, 16)
+    g.sync.wait_ge(S.stored, 16)
+
+    g.wait_ge(S.sent, n_sent[0])

@@ -1,8 +1,11 @@
-from concourse.bass import DstId, RemoteDMATransfer
 from concourse.mybir import dt, AluOpType, ActivationFunctionType
 
 NMAX = 192
 PAIRS = ("a", "b", "c", "d")
+LOADS = ("x", "w1", "w2")
+SENDS = (("xc", "even", "gotx"), ("w1c", "odd", "gotw1"), ("xs", "even", "gotx"),
+         ("ws", "even", "gotw1"), ("w2c", "odd", "gotw2"))
+YY = "all"
 
 SCRATCH = {
     "xin": ("sbuf", [128, 4 * NMAX], "bfloat16"),
@@ -24,8 +27,8 @@ for _n in PAIRS:
     SCRATCH["hq" + _n] = ("sbuf", [128, NMAX], "float8_e4m3fn_x4")
     SCRATCH["hs" + _n] = ("sbuf", [128, NMAX], "uint8")
 
-SEMAPHORES = ["lx", "lw1", "lw2", "qx", "qw1", "qw2", "sent", "gotx", "gotw1", "gotw2", "goty",
-              "ypdone", "ymdone", "ycopied", "ysummed", "stored"]
+SEMAPHORES = ["lx", "lw1", "lw2", "qx", "qw1", "qw2", "sent", "gotx", "gotw1", "gotw2", "goty0", "goty1",
+              "ypdone", "ymdone", "ycopied0", "ycopied1", "ysummed0", "ysummed1", "stored"]
 for _n in PAIRS:
     SEMAPHORES += ["z0" + _n, "z1" + _n, "h" + _n, "hq" + _n]
 
@@ -44,34 +47,51 @@ def rank_program(g, core, T, topo):
     n_m, n_p = wid[rank], wid[T.rank_of(partner)]
     u8 = dt.uint8
     n_sent = [0]
-    engines = {c: bin(topo.mask(core, c)).count("1") for c in (mate, partner)}
 
-    def send(dst, out, in_, sem):
+    def engines(dst, part):
+        m = topo.mask(core, dst)
+        es = [e for e in range(m.bit_length()) if m >> e & 1]
+        es = {"all": es, "even": es[0::2], "odd": es[1::2]}[part]
+        return sum(1 << e for e in es)
+
+    def count(dst, part):
+        return bin(engines(dst, part)).count("1")
+
+    def send(dst, part, out, in_, sem):
         rid, pid = topo.addr(dst, core)
-        g.remote_dma(out, in_, sem, S.sent, pid, rid, topo.mask(core, dst))
-        n_sent[0] += engines[dst]
+        g.remote_dma(out, in_, sem, S.sent, pid, rid, engines(dst, part))
+        n_sent[0] += count(dst, part)
 
-    g.sync.dma_start(T.xin[:, 0:4 * n_m], T.x[:, 0:4 * n_m]).then_inc(S.lx, 16)
-    g.sync.dma_start(T.win[:, 0:1024], T.w1[:, :]).then_inc(S.lw1, 16)
-    g.sync.dma_start(T.win[:, 1024:1536], T.w2[:, :]).then_inc(S.lw2, 16)
+    def halves(n):
+        return (slice(0, n // 2), slice(n // 2, n))
 
-    g.vector.wait_ge(S.lx, 16)
-    g.vector.quantize_mx(T.xq[:, 0:n_m], T.xs[:, 0:n_m], T.xin[:, 0:4 * n_m]).then_inc(S.qx, 1)
-    g.vector.wait_ge(S.lw1, 16)
-    g.vector.quantize_mx(T.wq[:, 0:256], T.ws[:, 0:256], T.win[:, 0:1024]).then_inc(S.qw1, 1)
-    g.vector.wait_ge(S.lw2, 16)
-    g.vector.quantize_mx(T.wq[:, 256:384], T.ws[:, 256:384], T.win[:, 1024:1536]).then_inc(S.qw2, 1)
+    src = {"x": (T.xin[:, 0:4 * n_m], T.x[:, 0:4 * n_m]), "w1": (T.win[:, 0:1024], T.w1[:, :]), "w2": (T.win[:, 1024:1536], T.w2[:, :])}
+    for k in LOADS:
+        g.sync.dma_start(src[k][0], src[k][1]).then_inc(S["l" + k], 16)
 
-    g.wait_ge(S.qx, 1)
-    send(partner, T.pq[:, 0:n_m].bitcast(u8), T.xq[:, 0:n_m].bitcast(u8), S.gotx)
-    send(partner, T.ps[:, 0:n_m], T.xs[:, 0:n_m], S.gotx)
-    g.wait_ge(S.qw1, 1)
-    send(mate, T.kq[:, 0:256].bitcast(u8), T.wq[:, 0:256].bitcast(u8), S.gotw1)
-    g.wait_ge(S.qw2, 1)
-    send(mate, T.ks[:, :], T.ws[:, :], S.gotw1)
-    send(mate, T.kq[:, 256:384].bitcast(u8), T.wq[:, 256:384].bitcast(u8), S.gotw2)
-    g.wait_ge(S.ycopied, 1)
-    send(partner, T.yland[:, 0:n_p], T.yout[:, 0:n_p], S.goty)
+    dst_q = {"x": (T.xq[:, 0:n_m], T.xs[:, 0:n_m]), "w1": (T.wq[:, 0:256], T.ws[:, 0:256]), "w2": (T.wq[:, 256:384], T.ws[:, 256:384])}
+    for k in LOADS:
+        g.vector.wait_ge(S["l" + k], 16)
+        g.vector.quantize_mx(dst_q[k][0], dst_q[k][1], src[k][0]).then_inc(S["q" + k], 1)
+
+    what = {"xc": (partner, T.pq[:, 0:n_m].bitcast(u8), T.xq[:, 0:n_m].bitcast(u8), ("qx",)),
+            "xs": (partner, T.ps[:, 0:n_m], T.xs[:, 0:n_m], ("qx",)),
+            "w1c": (mate, T.kq[:, 0:256].bitcast(u8), T.wq[:, 0:256].bitcast(u8), ("qw1",)),
+            "w2c": (mate, T.kq[:, 256:384].bitcast(u8), T.wq[:, 256:384].bitcast(u8), ("qw2",)),
+            "ws": (mate, T.ks[:, :], T.ws[:, :], ("qw1", "qw2"))}
+    waited = []
+    arrive = {}
+    for k, part, sem in SENDS:
+        dst, out, in_, needs = what[k]
+        for q in needs:
+            if q not in waited:
+                g.wait_ge(S[q], 1)
+                waited.append(q)
+        send(dst, part, out, in_, S[sem])
+        arrive[sem] = arrive.get(sem, 0) + count(dst, part)
+    for i, c in enumerate(halves(n_p)):
+        g.wait_ge(S["ycopied%d" % i], 1)
+        send(partner, YY, T.yland[:, c], T.yout[:, c], S["goty%d" % i])
 
     own_w, mate_w = (T.wq, T.ws), (T.kq, T.ks)
     own_x, part_x = (T.xq, T.xs, n_m), (T.pq, T.ps, n_p)
@@ -108,21 +128,22 @@ def rank_program(g, core, T, topo):
     first("a", own_w, own_x)
     g.tensor.wait_ge(S.qw2, 1)
     second("a", own_w, T.ym, n_m, True)
-    g.tensor.wait_ge(S.gotx, 2 * engines[partner])
+    g.tensor.wait_ge(S.gotx, arrive["gotx"])
     first("b", own_w, part_x)
-    second("b", own_w, T.yp, n_p, True)
-    g.tensor.wait_ge(S.gotw1, 2 * engines[mate])
+    g.tensor.wait_ge(S.gotw1, arrive["gotw1"])
     first("c", mate_w, part_x)
-    first("d", mate_w, own_x)
-    g.tensor.wait_ge(S.gotw2, engines[mate])
+    second("b", own_w, T.yp, n_p, True)
+    g.tensor.wait_ge(S.gotw2, arrive["gotw2"])
     second("c", mate_w, T.yp, n_p, False, S.ypdone)
+    first("d", mate_w, own_x)
     second("d", mate_w, T.ym, n_m, False, S.ymdone)
 
     act_scalar("a", n_m)
     act_scalar("b", n_p)
     act_scalar("c", n_p)
     g.scalar.wait_ge(S.ypdone, 1)
-    g.scalar.activation(T.yout[:, 0:n_p], T.yp[:, 0:n_p], ActivationFunctionType.Copy).then_inc(S.ycopied, 1)
+    for i, c in enumerate(halves(n_p)):
+        g.scalar.activation(T.yout[:, c], T.yp[:, c], ActivationFunctionType.Copy).then_inc(S["ycopied%d" % i], 1)
     act_scalar("d", n_m)
 
     act_vector("a", n_m)
@@ -130,11 +151,13 @@ def rank_program(g, core, T, topo):
     act_vector("c", n_p)
     act_vector("d", n_m)
     g.vector.wait_ge(S.ymdone, 1)
-    g.vector.wait_ge(S.goty, engines[partner])
-    g.vector.tensor_tensor(T.ysum[:, 0:n_m], T.ym[:, 0:n_m], T.yland[:, 0:n_m], AluOpType.add).then_inc(S.ysummed, 1)
+    for i, c in enumerate(halves(n_m)):
+        g.vector.wait_ge(S["goty%d" % i], count(partner, YY))
+        g.vector.tensor_tensor(T.ysum[:, c], T.ym[:, c], T.yland[:, c], AluOpType.add).then_inc(S["ysummed%d" % i], 1)
 
-    g.sync.wait_ge(S.ysummed, 1)
-    g.sync.dma_start(T.y[:, 0:n_m], T.ysum[:, 0:n_m]).then_inc(S.stored, 16)
-    g.sync.wait_ge(S.stored, 16)
+    for i, c in enumerate(halves(n_m)):
+        g.sync.wait_ge(S["ysummed%d" % i], 1)
+        g.sync.dma_start(T.y[:, c], T.ysum[:, c]).then_inc(S.stored, 16)
+    g.sync.wait_ge(S.stored, 32)
 
     g.wait_ge(S.sent, n_sent[0])

@@ -1,17 +1,16 @@
 from concourse.mybir import dt, AluOpType, ActivationFunctionType
 
 NMAX = 192
+HMAX = 256
 PAIRS = ("a", "b", "c", "d")
-LOADS = ("x", "w1", "w2")
-SENDS = (("xc", "even", "gotx"), ("w1c", "odd", "gotw1"), ("xs", "even", "gotx"),
-         ("ws", "even", "gotw1"), ("w2c", "odd", "gotw2"))
+SENDS = (("xs", "even", "gotxa"), ("xc0", "even", "gotxa"), ("w1c", "odd", "gotw1"), ("xc1", "even", "gotxb"),
+         ("ws", "odd", "gotw1"), ("w2c", "odd", "gotw2"))
 YY = "all"
 
 SCRATCH = {
     "xin": ("sbuf", [128, 4 * NMAX], "bfloat16"),
     "win": ("sbuf", [128, 1536], "bfloat16"),
-    "xq": ("sbuf", [128, NMAX], "float8_e4m3fn_x4"), "xs": ("sbuf", [128, NMAX], "uint8"),
-    "pq": ("sbuf", [128, NMAX], "float8_e4m3fn_x4"), "ps": ("sbuf", [128, NMAX], "uint8"),
+    "xq": ("sbuf", [128, 4 * NMAX], "float8_e4m3fn_x4"), "xs": ("sbuf", [128, 4 * NMAX], "uint8"),
     "wq": ("sbuf", [128, 384], "float8_e4m3fn_x4"), "ws": ("sbuf", [128, 384], "uint8"),
     "kq": ("sbuf", [128, 384], "float8_e4m3fn_x4"), "ks": ("sbuf", [128, 384], "uint8"),
     "yout": ("sbuf", [128, NMAX], "float32"),
@@ -20,15 +19,15 @@ SCRATCH = {
 }
 for _n in range(6):
     SCRATCH["z%d" % _n] = ("psum", [128, 512], "float32")
-for _n in ("ym", "yp"):
+for _n in ("ya", "yb"):
     SCRATCH[_n] = ("psum", [128, 512], "float32")
 for _n in PAIRS:
-    SCRATCH["h" + _n] = ("sbuf", [128, 4 * NMAX], "bfloat16")
-    SCRATCH["hq" + _n] = ("sbuf", [128, NMAX], "float8_e4m3fn_x4")
-    SCRATCH["hs" + _n] = ("sbuf", [128, NMAX], "uint8")
+    SCRATCH["h" + _n] = ("sbuf", [128, 4 * HMAX], "bfloat16")
+    SCRATCH["hq" + _n] = ("sbuf", [128, HMAX], "float8_e4m3fn_x4")
+    SCRATCH["hs" + _n] = ("sbuf", [128, HMAX], "uint8")
 
-SEMAPHORES = ["lx", "lw1", "lw2", "qx", "qw1", "qw2", "sent", "gotx", "gotw1", "gotw2", "goty0", "goty1",
-              "ypdone", "ymdone", "ycopied0", "ycopied1", "ysummed0", "ysummed1", "stored"]
+SEMAPHORES = ["lx", "lw1", "lw2", "qx", "qx2", "qw1", "qw2", "sent", "gotxa", "gotxb", "gotw1", "gotw2", "goty0", "goty1",
+              "yadone", "ybdone", "ycopied0", "ycopied1", "ysummed0", "ysummed1", "stored"]
 for _n in PAIRS:
     SEMAPHORES += ["z0" + _n, "z1" + _n, "h" + _n, "hq" + _n]
 
@@ -45,6 +44,10 @@ def rank_program(g, core, T, topo):
     mate = [c for c in others if topo.rack(topo.host(c)) == rack][0]
     partner = [c for c in others if topo.rack(topo.host(c)) != rack and topo.may_write(core, c)][0]
     n_m, n_p = wid[rank], wid[T.rank_of(partner)]
+    m2, p2 = n_m // 2, n_p // 2
+    n = m2 + p2
+    land = n_p
+    chunk_a, chunk_b = slice(m2, m2 + n), slice(m2 + n, m2 + 2 * n)
     u8 = dt.uint8
     n_sent = [0]
 
@@ -62,20 +65,22 @@ def rank_program(g, core, T, topo):
         g.remote_dma(out, in_, sem, S.sent, pid, rid, engines(dst, part))
         n_sent[0] += count(dst, part)
 
-    def halves(n):
-        return (slice(0, n // 2), slice(n // 2, n))
+    xin = T.xin[:, 0:4 * n_m]
+    g.sync.dma_start(xin, T.x[:, 0:4 * n_m]).then_inc(S.lx, 16)
+    g.sync.dma_start(T.win[:, 0:1024], T.w1[:, :]).then_inc(S.lw1, 16)
+    g.sync.dma_start(T.win[:, 1024:1536], T.w2[:, :]).then_inc(S.lw2, 16)
 
-    src = {"x": (T.xin[:, 0:4 * n_m], T.x[:, 0:4 * n_m]), "w1": (T.win[:, 0:1024], T.w1[:, :]), "w2": (T.win[:, 1024:1536], T.w2[:, :])}
-    for k in LOADS:
-        g.sync.dma_start(src[k][0], src[k][1]).then_inc(S["l" + k], 16)
+    g.vector.wait_ge(S.lx, 16)
+    g.vector.quantize_mx(T.xq[:, 0:n_m], T.xs[:, 0:n_m], xin).then_inc(S.qx, 1)
+    g.vector.wait_ge(S.lw1, 16)
+    g.vector.quantize_mx(T.wq[:, 0:256], T.ws[:, 0:256], T.win[:, 0:1024]).then_inc(S.qw1, 1)
+    g.vector.wait_ge(S.lw2, 16)
+    g.vector.quantize_mx(T.wq[:, 256:384], T.ws[:, 256:384], T.win[:, 1024:1536]).then_inc(S.qw2, 1)
+    g.vector.quantize_mx(T.xq[:, n_m + n_p:2 * n_m + n_p], T.xs[:, n_m + n_p:2 * n_m + n_p], xin).then_inc(S.qx2, 1)
 
-    dst_q = {"x": (T.xq[:, 0:n_m], T.xs[:, 0:n_m]), "w1": (T.wq[:, 0:256], T.ws[:, 0:256]), "w2": (T.wq[:, 256:384], T.ws[:, 256:384])}
-    for k in LOADS:
-        g.vector.wait_ge(S["l" + k], 16)
-        g.vector.quantize_mx(dst_q[k][0], dst_q[k][1], src[k][0]).then_inc(S["q" + k], 1)
-
-    what = {"xc": (partner, T.pq[:, 0:n_m].bitcast(u8), T.xq[:, 0:n_m].bitcast(u8), ("qx",)),
-            "xs": (partner, T.ps[:, 0:n_m], T.xs[:, 0:n_m], ("qx",)),
+    what = {"xs": (partner, T.xs[:, land:land + n_m], T.xs[:, 0:n_m], ("qx",)),
+            "xc0": (partner, T.xq[:, land:land + m2].bitcast(u8), T.xq[:, 0:m2].bitcast(u8), ("qx",)),
+            "xc1": (partner, T.xq[:, land + m2:land + n_m].bitcast(u8), T.xq[:, m2:n_m].bitcast(u8), ("qx",)),
             "w1c": (mate, T.kq[:, 0:256].bitcast(u8), T.wq[:, 0:256].bitcast(u8), ("qw1",)),
             "w2c": (mate, T.kq[:, 256:384].bitcast(u8), T.wq[:, 256:384].bitcast(u8), ("qw2",)),
             "ws": (mate, T.ks[:, :], T.ws[:, :], ("qw1", "qw2"))}
@@ -89,27 +94,26 @@ def rank_program(g, core, T, topo):
                 waited.append(q)
         send(dst, part, out, in_, S[sem])
         arrive[sem] = arrive.get(sem, 0) + count(dst, part)
-    for i, c in enumerate(halves(n_p)):
+    half_p, half_m = (slice(0, p2), slice(p2, n_p)), (slice(0, m2), slice(m2, n_m))
+    for i in range(2):
         g.wait_ge(S["ycopied%d" % i], 1)
-        send(partner, YY, T.yland[:, c], T.yout[:, c], S["goty%d" % i])
+        send(partner, YY, T.yland[:, half_p[i]], T.yout[:, half_p[i]], S["goty%d" % i])
 
     own_w, mate_w = (T.wq, T.ws), (T.kq, T.ks)
-    own_x, part_x = (T.xq, T.xs, n_m), (T.pq, T.ps, n_p)
     z_bank = {"a": (T.z0, T.z1), "b": (T.z2, T.z3), "c": (T.z4, T.z5), "d": (T.z0, T.z1)}
 
-    def first(p, w, x):
-        q, s, n = x
+    def first(p, w, c):
         for i in range(2):
             g.tensor.matmul_mx(z_bank[p][i][:, 0:n], w[0][:, 128 * i:128 * i + 128], w[1][:, 128 * i:128 * i + 128],
-                               q[:, 0:n], s[:, 0:n], True, True).then_inc(S["z%d%s" % (i, p)], 1)
+                               T.xq[:, c], T.xs[:, c], True, True).then_inc(S["z%d%s" % (i, p)], 1)
 
-    def act_scalar(p, n):
+    def act_scalar(p):
         h = T["h" + p]
         g.scalar.wait_ge(S["z0" + p], 1)
         for b, c in ((0, scale), (1, -scale)):
             g.scalar.activation(h[:, b:4 * n:4], z_bank[p][0][:, 0:n], ActivationFunctionType.Relu, scale=c).then_inc(S["h" + p], 1)
 
-    def act_vector(p, n):
+    def act_vector(p):
         h = T["h" + p]
         g.vector.wait_ge(S["z1" + p], 1)
         for b, c in ((2, scale), (3, -scale)):
@@ -117,7 +121,7 @@ def rank_program(g, core, T, topo):
         g.vector.wait_ge(S["h" + p], 4)
         g.vector.quantize_mx(T["hq" + p][:, 0:n], T["hs" + p][:, 0:n], h[:, 0:4 * n]).then_inc(S["hq" + p], 1)
 
-    def second(p, w, y, n, start, done=None):
+    def second(p, w, y, start, done=None):
         g.tensor.wait_ge(S["hq" + p], 1)
         r = g.tensor.matmul_mx(y[:, 0:n], w[0][:, 256:384], w[1][:, 256:384], T["hq" + p][:, 0:n], T["hs" + p][:, 0:n], start, not start)
         if done is not None:
@@ -125,39 +129,44 @@ def rank_program(g, core, T, topo):
 
     g.tensor.wait_ge(S.qx, 1)
     g.tensor.wait_ge(S.qw1, 1)
-    first("a", own_w, own_x)
-    g.tensor.wait_ge(S.qw2, 1)
-    second("a", own_w, T.ym, n_m, True)
-    g.tensor.wait_ge(S.gotx, arrive["gotx"])
-    first("b", own_w, part_x)
+    g.tensor.wait_ge(S.gotxa, arrive["gotxa"])
+    first("a", own_w, chunk_a)
     g.tensor.wait_ge(S.gotw1, arrive["gotw1"])
-    first("c", mate_w, part_x)
-    second("b", own_w, T.yp, n_p, True)
+    first("b", mate_w, chunk_a)
+    g.tensor.wait_ge(S.qw2, 1)
+    second("a", own_w, T.ya, True)
     g.tensor.wait_ge(S.gotw2, arrive["gotw2"])
-    second("c", mate_w, T.yp, n_p, False, S.ypdone)
-    first("d", mate_w, own_x)
-    second("d", mate_w, T.ym, n_m, False, S.ymdone)
+    second("b", mate_w, T.ya, False, S.yadone)
+    g.tensor.wait_ge(S.qx2, 1)
+    g.tensor.wait_ge(S.gotxb, arrive["gotxb"])
+    first("c", own_w, chunk_b)
+    first("d", mate_w, chunk_b)
+    second("c", own_w, T.yb, True)
+    second("d", mate_w, T.yb, False, S.ybdone)
 
-    act_scalar("a", n_m)
-    act_scalar("b", n_p)
-    act_scalar("c", n_p)
-    g.scalar.wait_ge(S.ypdone, 1)
-    for i, c in enumerate(halves(n_p)):
-        g.scalar.activation(T.yout[:, c], T.yp[:, c], ActivationFunctionType.Copy).then_inc(S["ycopied%d" % i], 1)
-    act_scalar("d", n_m)
+    act_scalar("a")
+    act_scalar("b")
+    g.scalar.wait_ge(S.yadone, 1)
+    g.scalar.activation(T.yout[:, half_p[0]], T.ya[:, m2:n], ActivationFunctionType.Copy).then_inc(S.ycopied0, 1)
+    act_scalar("c")
+    act_scalar("d")
+    g.scalar.wait_ge(S.ybdone, 1)
+    g.scalar.activation(T.yout[:, half_p[1]], T.yb[:, 0:p2], ActivationFunctionType.Copy).then_inc(S.ycopied1, 1)
 
-    act_vector("a", n_m)
-    act_vector("b", n_p)
-    act_vector("c", n_p)
-    act_vector("d", n_m)
-    g.vector.wait_ge(S.ymdone, 1)
-    for i, c in enumerate(halves(n_m)):
+    for p in PAIRS:
+        act_vector(p)
+    g.vector.wait_ge(S.yadone, 1)
+    g.vector.wait_ge(S.ybdone, 1)
+    g.vector.wait_ge(S.ycopied0, 1)
+    g.vector.wait_ge(S.ycopied1, 1)
+    own_y = (T.yb[:, p2:n], T.ya[:, 0:m2])
+    for i in range(2):
         g.vector.wait_ge(S["goty%d" % i], count(partner, YY))
-        g.vector.tensor_tensor(T.ysum[:, c], T.ym[:, c], T.yland[:, c], AluOpType.add).then_inc(S["ysummed%d" % i], 1)
+        g.vector.tensor_tensor(T.ysum[:, half_m[i]], own_y[i], T.yland[:, half_m[i]], AluOpType.add).then_inc(S["ysummed%d" % i], 1)
 
-    for i, c in enumerate(halves(n_m)):
+    for i in range(2):
         g.sync.wait_ge(S["ysummed%d" % i], 1)
-        g.sync.dma_start(T.y[:, c], T.ysum[:, c]).then_inc(S.stored, 16)
+        g.sync.dma_start(T.y[:, half_m[i]], T.ysum[:, half_m[i]]).then_inc(S.stored, 16)
     g.sync.wait_ge(S.stored, 32)
 
     g.wait_ge(S.sent, n_sent[0])

@@ -1,69 +1,129 @@
 from concourse.mybir import dt, AluOpType, ActivationFunctionType
 
 NMAX = 192
-HMAX = 256
-PAIRS = ("a", "b", "c", "d")
-SENDS = (("xs", "even", "gotxa"), ("xc0", "even", "gotxa"), ("w1c", "odd", "gotw1"), ("xc1", "even", "gotxb"),
-         ("ws", "odd", "gotw1"), ("w2c", "odd", "gotw2"))
-YY = "all"
+XCUT = (("x1", "codes", 0, 0.26, "a"), ("x2", "codes", 0.26, 0.42, "c"), ("xs", "scales", 0, 1, "d"), ("x0", "codes", 0.42, 1, "d"))
+YCUT = ((0.3, "d"), (0.22, "a"), (0.3, "d"), (0.18, "c"))
+WCUT = (("w1", "codes", 0, 256, "d", "gotw1"), ("ws", "scales", 0, 384, "d", "gotw1"), ("w2", "codes", 256, 384, "b", "gotw2"))
+ORDER = ("x1", "x2", "xs", "w1", "x0", "w2", "ws")
+ENGINES = {"x": "even", "w": "odd", "y": "all", "hand": "chip", "carry": "all"}
 
 SCRATCH = {
     "xin": ("sbuf", [128, 4 * NMAX], "bfloat16"),
     "win": ("sbuf", [128, 1536], "bfloat16"),
-    "xq": ("sbuf", [128, 4 * NMAX], "float8_e4m3fn_x4"), "xs": ("sbuf", [128, 4 * NMAX], "uint8"),
+    "xq": ("sbuf", [128, 2 * NMAX], "float8_e4m3fn_x4"), "xs": ("sbuf", [128, 2 * NMAX], "uint8"),
     "wq": ("sbuf", [128, 384], "float8_e4m3fn_x4"), "ws": ("sbuf", [128, 384], "uint8"),
     "kq": ("sbuf", [128, 384], "float8_e4m3fn_x4"), "ks": ("sbuf", [128, 384], "uint8"),
     "yout": ("sbuf", [128, NMAX], "float32"),
     "yland": ("sbuf", [128, NMAX], "float32"),
     "ysum": ("sbuf", [128, NMAX], "float32"),
 }
+PAIRS = ("om", "op", "mp", "mm")
 for _n in range(6):
     SCRATCH["z%d" % _n] = ("psum", [128, 512], "float32")
-for _n in ("ya", "yb"):
+for _n in ("yp", "ym"):
     SCRATCH[_n] = ("psum", [128, 512], "float32")
 for _n in PAIRS:
-    SCRATCH["h" + _n] = ("sbuf", [128, 4 * HMAX], "bfloat16")
-    SCRATCH["hq" + _n] = ("sbuf", [128, HMAX], "float8_e4m3fn_x4")
-    SCRATCH["hs" + _n] = ("sbuf", [128, HMAX], "uint8")
+    SCRATCH["h" + _n] = ("sbuf", [128, 4 * NMAX], "bfloat16")
+    SCRATCH["hq" + _n] = ("sbuf", [128, NMAX], "float8_e4m3fn_x4")
+    SCRATCH["hs" + _n] = ("sbuf", [128, NMAX], "uint8")
 
-SEMAPHORES = ["lx", "lw1", "lw2", "qx", "qx2", "qw1", "qw2", "sent", "gotxa", "gotxb", "gotw1", "gotw2", "goty0", "goty1",
-              "yadone", "ybdone", "ycopied0", "ycopied1", "ysummed0", "ysummed1", "stored"]
+SEMAPHORES = ["lx", "lw1", "lw2", "qx", "qw1", "qw2", "sent", "gotx", "gotw1", "gotw2", "ypdone", "ymdone", "stored"]
+SEMAPHORES += ["at" + w[0] for w in WCUT] + ["at" + x[0] for x in XCUT]
+for _n in range(len(YCUT)):
+    SEMAPHORES += ["goty%d" % _n, "aty%d" % _n, "ycopied%d" % _n, "ysummed%d" % _n]
 for _n in PAIRS:
     SEMAPHORES += ["z0" + _n, "z1" + _n, "h" + _n, "hq" + _n]
 
 
 def rank_program(g, core, T, topo):
-    rank = T.rank_of(core)
-    if rank is None:
-        return
     S = T.sem
     wid = T.tables["WID"]
     scale = 0.043
-    rack = topo.rack(topo.host(core))
-    others = [c for c in T.cores if c != core]
-    mate = [c for c in others if topo.rack(topo.host(c)) == rack][0]
-    partner = [c for c in others if topo.rack(topo.host(c)) != rack and topo.may_write(core, c)][0]
-    n_m, n_p = wid[rank], wid[T.rank_of(partner)]
-    m2, p2 = n_m // 2, n_p // 2
-    n = m2 + p2
-    land = n_p
-    chunk_a, chunk_b = slice(m2, m2 + n), slice(m2 + n, m2 + 2 * n)
     u8 = dt.uint8
+    one_chip = lambda c, d: topo.host(c) == topo.host(d) and topo.chip(c) == topo.chip(d)
+    here = [c for c in T.cores if one_chip(c, core)]
+    if not here:
+        return
+    home = here[0]
+    rack = topo.rack(topo.host(home))
+    others = [c for c in T.cores if c != home]
+    mate = [c for c in others if topo.rack(topo.host(c)) == rack][0]
+    partner = [c for c in others if topo.rack(topo.host(c)) != rack and topo.may_write(home, c)][0]
+    n_m, n_p = wid[T.rank_of(home)], wid[T.rank_of(partner)]
+
+    reach = [c for c in range(max(0, home - 64), home + 64) if topo.host(c) == topo.host(home)]
+    chip = [c for c in reach if one_chip(c, home)]
+    beside = [c for c in reach if topo.mates(home, c)]
+    owns = lambda c: all(topo.may_write(c, x) for x in beside)
+    pick = lambda same_die, same_pair: [c for c in chip if c != home and (topo.die(c) == topo.die(home)) == same_die
+                                        and (owns(c) == owns(home)) == same_pair][0]
+    role = {"d": home, "a": pick(True, False), "b": pick(False, True), "c": pick(False, False)}
+
+    off_chip = topo.mask(home, partner)
     n_sent = [0]
 
-    def engines(dst, part):
-        m = topo.mask(core, dst)
+    def engines(src, dst, part):
+        m = topo.mask(src, dst)
         es = [e for e in range(m.bit_length()) if m >> e & 1]
-        es = {"all": es, "even": es[0::2], "odd": es[1::2]}[part]
+        es = {"all": es, "even": es[0::2], "odd": es[1::2], "chip": [e for e in es if not off_chip >> e & 1]}[part]
         return sum(1 << e for e in es)
 
-    def count(dst, part):
-        return bin(engines(dst, part)).count("1")
+    def count(src, dst, part):
+        return bin(engines(src, dst, part)).count("1")
 
     def send(dst, part, out, in_, sem):
         rid, pid = topo.addr(dst, core)
-        g.remote_dma(out, in_, sem, S.sent, pid, rid, engines(dst, part))
-        n_sent[0] += count(dst, part)
+        g.remote_dma(out, in_, sem, S.sent, pid, rid, engines(core, dst, part))
+        n_sent[0] += count(core, dst, part)
+
+    def cuts(n):
+        ends = [0]
+        for f, _ in YCUT:
+            ends.append(ends[-1] + f)
+        ends = [int(round(n * e / 4)) * 4 for e in ends[:-1]] + [n]
+        return [(a, b, r) for a, b, (_, r) in zip(ends, ends[1:], YCUT)]
+
+    yout, yin = cuts(n_p), cuts(n_m)
+    land = NMAX
+
+    def codes(buf, a, b):
+        return buf[:, a:b].bitcast(u8)
+
+    xcut = []
+    for k, kind, f, t, r in XCUT:
+        a, b = [int(round(n_m * e / 8)) * 8 for e in (f, t)]
+        if kind == "codes":
+            xcut.append((k, r, codes(T.xq, land + a, land + b), codes(T.xq, a, b)))
+        else:
+            xcut.append((k, r, T.xs[:, land + a:land + b], T.xs[:, a:b]))
+    wcut = []
+    for k, kind, a, b, r, sem in WCUT:
+        needs = tuple(q for q, used in (("qw1", a < 256), ("qw2", b > 256)) if used)
+        out, in_ = (codes(T.kq, a, b), codes(T.wq, a, b)) if kind == "codes" else (T.ks[:, a:b], T.ws[:, a:b])
+        wcut.append((k, r, out, in_, needs, sem))
+
+    if core != home:
+        mine = [k for k in role if role[k] == core]
+        if not mine:
+            return
+        jobs = {}
+        for k, r, out, in_ in xcut:
+            if r == mine[0]:
+                jobs[k] = (partner, out, in_, "gotx")
+        for k, r, out, in_, needs, sem in wcut:
+            if r == mine[0]:
+                jobs[k] = (mate, out, in_, sem)
+        for i, (a, b, r) in enumerate(yout):
+            if r == mine[0]:
+                jobs["y%d" % i] = (partner, T.yland[:, a:b], T.yout[:, a:b], "goty%d" % i)
+        for k in ORDER + tuple("y%d" % i for i in range(len(yout))):
+            if k in jobs:
+                dst, out, in_, sem = jobs[k]
+                g.wait_ge(S["at" + k], count(home, core, ENGINES["hand"]))
+                send(dst, ENGINES["carry"], out, in_, S[sem])
+        if jobs:
+            g.wait_ge(S.sent, n_sent[0])
+        return
 
     xin = T.xin[:, 0:4 * n_m]
     g.sync.dma_start(xin, T.x[:, 0:4 * n_m]).then_inc(S.lx, 16)
@@ -76,52 +136,68 @@ def rank_program(g, core, T, topo):
     g.vector.quantize_mx(T.wq[:, 0:256], T.ws[:, 0:256], T.win[:, 0:1024]).then_inc(S.qw1, 1)
     g.vector.wait_ge(S.lw2, 16)
     g.vector.quantize_mx(T.wq[:, 256:384], T.ws[:, 256:384], T.win[:, 1024:1536]).then_inc(S.qw2, 1)
-    g.vector.quantize_mx(T.xq[:, n_m + n_p:2 * n_m + n_p], T.xs[:, n_m + n_p:2 * n_m + n_p], xin).then_inc(S.qx2, 1)
 
-    what = {"xs": (partner, T.xs[:, land:land + n_m], T.xs[:, 0:n_m], ("qx",)),
-            "xc0": (partner, T.xq[:, land:land + m2].bitcast(u8), T.xq[:, 0:m2].bitcast(u8), ("qx",)),
-            "xc1": (partner, T.xq[:, land + m2:land + n_m].bitcast(u8), T.xq[:, m2:n_m].bitcast(u8), ("qx",)),
-            "w1c": (mate, T.kq[:, 0:256].bitcast(u8), T.wq[:, 0:256].bitcast(u8), ("qw1",)),
-            "w2c": (mate, T.kq[:, 256:384].bitcast(u8), T.wq[:, 256:384].bitcast(u8), ("qw2",)),
-            "ws": (mate, T.ks[:, :], T.ws[:, :], ("qw1", "qw2"))}
+    n_x, n_w = count(role["a"], partner, ENGINES["carry"]), count(role["b"], mate, ENGINES["carry"])
+    arrive = {"gotx": 0, "gotw1": 0, "gotw2": 0}
+    what = {}
+    for k, r, out, in_ in xcut:
+        if r == "d":
+            what[k] = (partner, ENGINES["x"], out, in_, ("qx",), "gotx")
+            arrive["gotx"] += count(core, partner, ENGINES["x"])
+        else:
+            what[k] = (role[r], ENGINES["hand"], in_, in_, ("qx",), "at" + k)
+            arrive["gotx"] += n_x
+    for k, r, out, in_, needs, sem in wcut:
+        if r == "d":
+            what[k] = (mate, ENGINES["w"], out, in_, needs, sem)
+            arrive[sem] += count(core, mate, ENGINES["w"])
+        else:
+            what[k] = (role[r], ENGINES["hand"], in_, in_, needs, "at" + k)
+            arrive[sem] += n_w
     waited = []
-    arrive = {}
-    for k, part, sem in SENDS:
-        dst, out, in_, needs = what[k]
+    for k in ORDER:
+        dst, part, out, in_, needs, sem = what[k]
         for q in needs:
             if q not in waited:
                 g.wait_ge(S[q], 1)
                 waited.append(q)
         send(dst, part, out, in_, S[sem])
-        arrive[sem] = arrive.get(sem, 0) + count(dst, part)
-    half_p, half_m = (slice(0, p2), slice(p2, n_p)), (slice(0, m2), slice(m2, n_m))
-    for i in range(2):
+    for i, (a, b, r) in enumerate(yout):
         g.wait_ge(S["ycopied%d" % i], 1)
-        send(partner, YY, T.yland[:, half_p[i]], T.yout[:, half_p[i]], S["goty%d" % i])
+        if r == "d":
+            send(partner, ENGINES["y"], T.yland[:, a:b], T.yout[:, a:b], S["goty%d" % i])
+        else:
+            send(role[r], ENGINES["hand"], T.yout[:, a:b], T.yout[:, a:b], S["aty%d" % i])
 
     own_w, mate_w = (T.wq, T.ws), (T.kq, T.ks)
-    z_bank = {"a": (T.z0, T.z1), "b": (T.z2, T.z3), "c": (T.z4, T.z5), "d": (T.z0, T.z1)}
+    cm, cp = slice(0, n_m), slice(land, land + n_p)
+    z_bank = {"om": (T.z0, T.z1), "op": (T.z2, T.z3), "mp": (T.z4, T.z5), "mm": (T.z0, T.z1)}
+    width = {"om": n_m, "op": n_p, "mp": n_p, "mm": n_m}
 
     def first(p, w, c):
         for i in range(2):
-            g.tensor.matmul_mx(z_bank[p][i][:, 0:n], w[0][:, 128 * i:128 * i + 128], w[1][:, 128 * i:128 * i + 128],
+            g.tensor.matmul_mx(z_bank[p][i][:, 0:width[p]], w[0][:, 128 * i:128 * i + 128], w[1][:, 128 * i:128 * i + 128],
                                T.xq[:, c], T.xs[:, c], True, True).then_inc(S["z%d%s" % (i, p)], 1)
 
-    def act_scalar(p):
-        h = T["h" + p]
-        g.scalar.wait_ge(S["z0" + p], 1)
-        for b, c in ((0, scale), (1, -scale)):
-            g.scalar.activation(h[:, b:4 * n:4], z_bank[p][0][:, 0:n], ActivationFunctionType.Relu, scale=c).then_inc(S["h" + p], 1)
-
     def act_vector(p):
-        h = T["h" + p]
-        g.vector.wait_ge(S["z1" + p], 1)
+        h, n = T["h" + p], width[p]
+        g.vector.wait_ge(S["z0" + p], 1)
+        for b, c in ((0, scale), (1, -scale)):
+            g.vector.tensor_scalar(h[:, b:4 * n:4], z_bank[p][0][:, 0:n], c, 0.0, AluOpType.mult, AluOpType.max).then_inc(S["h" + p], 1)
+
+    def act_scalar(p):
+        h, n = T["h" + p], width[p]
+        g.scalar.wait_ge(S["z1" + p], 1)
         for b, c in ((2, scale), (3, -scale)):
-            g.vector.tensor_scalar(h[:, b:4 * n:4], z_bank[p][1][:, 0:n], c, 0.0, AluOpType.mult, AluOpType.max).then_inc(S["h" + p], 1)
+            g.scalar.activation(h[:, b:4 * n:4], z_bank[p][1][:, 0:n], ActivationFunctionType.Relu, scale=c).then_inc(S["h" + p], 1)
+
+    def pack(p):
+        h, n = T["h" + p], width[p]
         g.vector.wait_ge(S["h" + p], 4)
         g.vector.quantize_mx(T["hq" + p][:, 0:n], T["hs" + p][:, 0:n], h[:, 0:4 * n]).then_inc(S["hq" + p], 1)
 
     def second(p, w, y, start, done=None):
+        n = width[p]
         g.tensor.wait_ge(S["hq" + p], 1)
         r = g.tensor.matmul_mx(y[:, 0:n], w[0][:, 256:384], w[1][:, 256:384], T["hq" + p][:, 0:n], T["hs" + p][:, 0:n], start, not start)
         if done is not None:
@@ -129,44 +205,42 @@ def rank_program(g, core, T, topo):
 
     g.tensor.wait_ge(S.qx, 1)
     g.tensor.wait_ge(S.qw1, 1)
-    g.tensor.wait_ge(S.gotxa, arrive["gotxa"])
-    first("a", own_w, chunk_a)
-    g.tensor.wait_ge(S.gotw1, arrive["gotw1"])
-    first("b", mate_w, chunk_a)
+    first("om", own_w, cm)
     g.tensor.wait_ge(S.qw2, 1)
-    second("a", own_w, T.ya, True)
+    second("om", own_w, T.ym, True)
+    g.tensor.wait_ge(S.gotx, arrive["gotx"])
+    first("op", own_w, cp)
+    g.tensor.wait_ge(S.gotw1, arrive["gotw1"])
+    first("mp", mate_w, cp)
+    first("mm", mate_w, cm)
+    second("op", own_w, T.yp, True)
     g.tensor.wait_ge(S.gotw2, arrive["gotw2"])
-    second("b", mate_w, T.ya, False, S.yadone)
-    g.tensor.wait_ge(S.qx2, 1)
-    g.tensor.wait_ge(S.gotxb, arrive["gotxb"])
-    first("c", own_w, chunk_b)
-    first("d", mate_w, chunk_b)
-    second("c", own_w, T.yb, True)
-    second("d", mate_w, T.yb, False, S.ybdone)
+    second("mp", mate_w, T.yp, False, S.ypdone)
+    second("mm", mate_w, T.ym, False, S.ymdone)
 
-    act_scalar("a")
-    act_scalar("b")
-    g.scalar.wait_ge(S.yadone, 1)
-    g.scalar.activation(T.yout[:, half_p[0]], T.ya[:, m2:n], ActivationFunctionType.Copy).then_inc(S.ycopied0, 1)
-    act_scalar("c")
-    act_scalar("d")
-    g.scalar.wait_ge(S.ybdone, 1)
-    g.scalar.activation(T.yout[:, half_p[1]], T.yb[:, 0:p2], ActivationFunctionType.Copy).then_inc(S.ycopied1, 1)
+    for p in ("om", "op", "mp"):
+        act_scalar(p)
+    g.scalar.wait_ge(S.ypdone, 1)
+    for i, (a, b, r) in enumerate(yout):
+        g.scalar.activation(T.yout[:, a:b], T.yp[:, a:b], ActivationFunctionType.Copy).then_inc(S["ycopied%d" % i], 1)
+    act_scalar("mm")
 
-    for p in PAIRS:
-        act_vector(p)
-    g.vector.wait_ge(S.yadone, 1)
-    g.vector.wait_ge(S.ybdone, 1)
-    g.vector.wait_ge(S.ycopied0, 1)
-    g.vector.wait_ge(S.ycopied1, 1)
-    own_y = (T.yb[:, p2:n], T.ya[:, 0:m2])
-    for i in range(2):
-        g.vector.wait_ge(S["goty%d" % i], count(partner, YY))
-        g.vector.tensor_tensor(T.ysum[:, half_m[i]], own_y[i], T.yland[:, half_m[i]], AluOpType.add).then_inc(S["ysummed%d" % i], 1)
+    act_vector("om")
+    pack("om")
+    act_vector("op")
+    act_vector("mp")
+    pack("op")
+    pack("mp")
+    act_vector("mm")
+    pack("mm")
+    g.vector.wait_ge(S.ymdone, 1)
+    for i, (a, b, r) in enumerate(yin):
+        g.vector.wait_ge(S["goty%d" % i], count(role[r], partner, ENGINES["y" if r == "d" else "carry"]))
+        g.vector.tensor_tensor(T.ysum[:, a:b], T.ym[:, a:b], T.yland[:, a:b], AluOpType.add).then_inc(S["ysummed%d" % i], 1)
 
-    for i in range(2):
+    for i, (a, b, r) in enumerate(yin):
         g.sync.wait_ge(S["ysummed%d" % i], 1)
-        g.sync.dma_start(T.y[:, half_m[i]], T.ysum[:, half_m[i]]).then_inc(S.stored, 16)
-    g.sync.wait_ge(S.stored, 32)
+        g.sync.dma_start(T.y[:, a:b], T.ysum[:, a:b]).then_inc(S.stored, 16)
+    g.sync.wait_ge(S.stored, 16 * len(yin))
 
     g.wait_ge(S.sent, n_sent[0])

from concourse.mybir import dt, AluOpType, ActivationFunctionType

NMAX = 192
XCUT = (("x1", "codes", 0, 0.26, "a"), ("x2", "codes", 0.26, 0.42, "c"), ("xs", "scales", 0, 1, "d"), ("x0", "codes", 0.42, 1, "d"))
YCUT = ((0.3, "d"), (0.22, "a"), (0.3, "d"), (0.18, "c"))
WCUT = (("w1", "codes", 0, 256, "d", "gotw1"), ("ws", "scales", 0, 384, "d", "gotw1"), ("w2", "codes", 256, 384, "b", "gotw2"))
ORDER = ("x1", "x2", "xs", "w1", "x0", "w2", "ws")
ENGINES = {"x": "even", "w": "odd", "y": "all", "hand": "chip", "carry": "all"}

SCRATCH = {
    "xin": ("sbuf", [128, 4 * NMAX], "bfloat16"),
    "win": ("sbuf", [128, 1536], "bfloat16"),
    "xq": ("sbuf", [128, 2 * NMAX], "float8_e4m3fn_x4"), "xs": ("sbuf", [128, 2 * NMAX], "uint8"),
    "wq": ("sbuf", [128, 384], "float8_e4m3fn_x4"), "ws": ("sbuf", [128, 384], "uint8"),
    "kq": ("sbuf", [128, 384], "float8_e4m3fn_x4"), "ks": ("sbuf", [128, 384], "uint8"),
    "yout": ("sbuf", [128, NMAX], "float32"),
    "yland": ("sbuf", [128, NMAX], "float32"),
    "ysum": ("sbuf", [128, NMAX], "float32"),
}
PAIRS = ("om", "op", "mp", "mm")
for _n in range(6):
    SCRATCH["z%d" % _n] = ("psum", [128, 512], "float32")
for _n in ("yp", "ym"):
    SCRATCH[_n] = ("psum", [128, 512], "float32")
for _n in PAIRS:
    SCRATCH["h" + _n] = ("sbuf", [128, 4 * NMAX], "bfloat16")
    SCRATCH["hq" + _n] = ("sbuf", [128, NMAX], "float8_e4m3fn_x4")
    SCRATCH["hs" + _n] = ("sbuf", [128, NMAX], "uint8")

SEMAPHORES = ["lx", "lw1", "lw2", "qx", "qw1", "qw2", "sent", "gotx", "gotw1", "gotw2", "ypdone", "ymdone", "stored"]
SEMAPHORES += ["at" + w[0] for w in WCUT] + ["at" + x[0] for x in XCUT]
for _n in range(len(YCUT)):
    SEMAPHORES += ["goty%d" % _n, "aty%d" % _n, "ycopied%d" % _n, "ysummed%d" % _n]
for _n in PAIRS:
    SEMAPHORES += ["z0" + _n, "z1" + _n, "h" + _n, "hq" + _n]


def rank_program(g, core, T, topo):
    S = T.sem
    wid = T.tables["WID"]
    scale = 0.043
    u8 = dt.uint8
    one_chip = lambda c, d: topo.host(c) == topo.host(d) and topo.chip(c) == topo.chip(d)
    here = [c for c in T.cores if one_chip(c, core)]
    if not here:
        return
    home = here[0]
    rack = topo.rack(topo.host(home))
    others = [c for c in T.cores if c != home]
    mate = [c for c in others if topo.rack(topo.host(c)) == rack][0]
    partner = [c for c in others if topo.rack(topo.host(c)) != rack and topo.may_write(home, c)][0]
    n_m, n_p = wid[T.rank_of(home)], wid[T.rank_of(partner)]

    reach = [c for c in range(max(0, home - 64), home + 64) if topo.host(c) == topo.host(home)]
    chip = [c for c in reach if one_chip(c, home)]
    beside = [c for c in reach if topo.mates(home, c)]
    owns = lambda c: all(topo.may_write(c, x) for x in beside)
    pick = lambda same_die, same_pair: [c for c in chip if c != home and (topo.die(c) == topo.die(home)) == same_die
                                        and (owns(c) == owns(home)) == same_pair][0]
    role = {"d": home, "a": pick(True, False), "b": pick(False, True), "c": pick(False, False)}

    off_chip = topo.mask(home, partner)
    n_sent = [0]

    def engines(src, dst, part):
        m = topo.mask(src, dst)
        es = [e for e in range(m.bit_length()) if m >> e & 1]
        es = {"all": es, "even": es[0::2], "odd": es[1::2], "chip": [e for e in es if not off_chip >> e & 1]}[part]
        return sum(1 << e for e in es)

    def count(src, dst, part):
        return bin(engines(src, dst, part)).count("1")

    def send(dst, part, out, in_, sem):
        rid, pid = topo.addr(dst, core)
        g.remote_dma(out, in_, sem, S.sent, pid, rid, engines(core, dst, part))
        n_sent[0] += count(core, dst, part)

    def cuts(n):
        ends = [0]
        for f, _ in YCUT:
            ends.append(ends[-1] + f)
        ends = [int(round(n * e / 4)) * 4 for e in ends[:-1]] + [n]
        return [(a, b, r) for a, b, (_, r) in zip(ends, ends[1:], YCUT)]

    yout, yin = cuts(n_p), cuts(n_m)
    land = NMAX

    def codes(buf, a, b):
        return buf[:, a:b].bitcast(u8)

    xcut = []
    for k, kind, f, t, r in XCUT:
        a, b = [int(round(n_m * e / 8)) * 8 for e in (f, t)]
        if kind == "codes":
            xcut.append((k, r, codes(T.xq, land + a, land + b), codes(T.xq, a, b)))
        else:
            xcut.append((k, r, T.xs[:, land + a:land + b], T.xs[:, a:b]))
    wcut = []
    for k, kind, a, b, r, sem in WCUT:
        needs = tuple(q for q, used in (("qw1", a < 256), ("qw2", b > 256)) if used)
        out, in_ = (codes(T.kq, a, b), codes(T.wq, a, b)) if kind == "codes" else (T.ks[:, a:b], T.ws[:, a:b])
        wcut.append((k, r, out, in_, needs, sem))

    if core != home:
        mine = [k for k in role if role[k] == core]
        if not mine:
            return
        jobs = {}
        for k, r, out, in_ in xcut:
            if r == mine[0]:
                jobs[k] = (partner, out, in_, "gotx")
        for k, r, out, in_, needs, sem in wcut:
            if r == mine[0]:
                jobs[k] = (mate, out, in_, sem)
        for i, (a, b, r) in enumerate(yout):
            if r == mine[0]:
                jobs["y%d" % i] = (partner, T.yland[:, a:b], T.yout[:, a:b], "goty%d" % i)
        for k in ORDER + tuple("y%d" % i for i in range(len(yout))):
            if k in jobs:
                dst, out, in_, sem = jobs[k]
                g.wait_ge(S["at" + k], count(home, core, ENGINES["hand"]))
                send(dst, ENGINES["carry"], out, in_, S[sem])
        if jobs:
            g.wait_ge(S.sent, n_sent[0])
        return

    xin = T.xin[:, 0:4 * n_m]
    g.sync.dma_start(xin, T.x[:, 0:4 * n_m]).then_inc(S.lx, 16)
    g.sync.dma_start(T.win[:, 0:1024], T.w1[:, :]).then_inc(S.lw1, 16)
    g.sync.dma_start(T.win[:, 1024:1536], T.w2[:, :]).then_inc(S.lw2, 16)

    g.vector.wait_ge(S.lx, 16)
    g.vector.quantize_mx(T.xq[:, 0:n_m], T.xs[:, 0:n_m], xin).then_inc(S.qx, 1)
    g.vector.wait_ge(S.lw1, 16)
    g.vector.quantize_mx(T.wq[:, 0:256], T.ws[:, 0:256], T.win[:, 0:1024]).then_inc(S.qw1, 1)
    g.vector.wait_ge(S.lw2, 16)
    g.vector.quantize_mx(T.wq[:, 256:384], T.ws[:, 256:384], T.win[:, 1024:1536]).then_inc(S.qw2, 1)

    n_x, n_w = count(role["a"], partner, ENGINES["carry"]), count(role["b"], mate, ENGINES["carry"])
    arrive = {"gotx": 0, "gotw1": 0, "gotw2": 0}
    what = {}
    for k, r, out, in_ in xcut:
        if r == "d":
            what[k] = (partner, ENGINES["x"], out, in_, ("qx",), "gotx")
            arrive["gotx"] += count(core, partner, ENGINES["x"])
        else:
            what[k] = (role[r], ENGINES["hand"], in_, in_, ("qx",), "at" + k)
            arrive["gotx"] += n_x
    for k, r, out, in_, needs, sem in wcut:
        if r == "d":
            what[k] = (mate, ENGINES["w"], out, in_, needs, sem)
            arrive[sem] += count(core, mate, ENGINES["w"])
        else:
            what[k] = (role[r], ENGINES["hand"], in_, in_, needs, "at" + k)
            arrive[sem] += n_w
    waited = []
    for k in ORDER:
        dst, part, out, in_, needs, sem = what[k]
        for q in needs:
            if q not in waited:
                g.wait_ge(S[q], 1)
                waited.append(q)
        send(dst, part, out, in_, S[sem])
    for i, (a, b, r) in enumerate(yout):
        g.wait_ge(S["ycopied%d" % i], 1)
        if r == "d":
            send(partner, ENGINES["y"], T.yland[:, a:b], T.yout[:, a:b], S["goty%d" % i])
        else:
            send(role[r], ENGINES["hand"], T.yout[:, a:b], T.yout[:, a:b], S["aty%d" % i])

    own_w, mate_w = (T.wq, T.ws), (T.kq, T.ks)
    cm, cp = slice(0, n_m), slice(land, land + n_p)
    z_bank = {"om": (T.z0, T.z1), "op": (T.z2, T.z3), "mp": (T.z4, T.z5), "mm": (T.z0, T.z1)}
    width = {"om": n_m, "op": n_p, "mp": n_p, "mm": n_m}

    def first(p, w, c):
        for i in range(2):
            g.tensor.matmul_mx(z_bank[p][i][:, 0:width[p]], w[0][:, 128 * i:128 * i + 128], w[1][:, 128 * i:128 * i + 128],
                               T.xq[:, c], T.xs[:, c], True, True).then_inc(S["z%d%s" % (i, p)], 1)

    def act_vector(p):
        h, n = T["h" + p], width[p]
        g.vector.wait_ge(S["z0" + p], 1)
        for b, c in ((0, scale), (1, -scale)):
            g.vector.tensor_scalar(h[:, b:4 * n:4], z_bank[p][0][:, 0:n], c, 0.0, AluOpType.mult, AluOpType.max).then_inc(S["h" + p], 1)

    def act_scalar(p):
        h, n = T["h" + p], width[p]
        g.scalar.wait_ge(S["z1" + p], 1)
        for b, c in ((2, scale), (3, -scale)):
            g.scalar.activation(h[:, b:4 * n:4], z_bank[p][1][:, 0:n], ActivationFunctionType.Relu, scale=c).then_inc(S["h" + p], 1)

    def pack(p):
        h, n = T["h" + p], width[p]
        g.vector.wait_ge(S["h" + p], 4)
        g.vector.quantize_mx(T["hq" + p][:, 0:n], T["hs" + p][:, 0:n], h[:, 0:4 * n]).then_inc(S["hq" + p], 1)

    def second(p, w, y, start, done=None):
        n = width[p]
        g.tensor.wait_ge(S["hq" + p], 1)
        r = g.tensor.matmul_mx(y[:, 0:n], w[0][:, 256:384], w[1][:, 256:384], T["hq" + p][:, 0:n], T["hs" + p][:, 0:n], start, not start)
        if done is not None:
            r.then_inc(done, 1)

    g.tensor.wait_ge(S.qx, 1)
    g.tensor.wait_ge(S.qw1, 1)
    first("om", own_w, cm)
    g.tensor.wait_ge(S.qw2, 1)
    second("om", own_w, T.ym, True)
    g.tensor.wait_ge(S.gotx, arrive["gotx"])
    first("op", own_w, cp)
    g.tensor.wait_ge(S.gotw1, arrive["gotw1"])
    first("mp", mate_w, cp)
    first("mm", mate_w, cm)
    second("op", own_w, T.yp, True)
    g.tensor.wait_ge(S.gotw2, arrive["gotw2"])
    second("mp", mate_w, T.yp, False, S.ypdone)
    second("mm", mate_w, T.ym, False, S.ymdone)

    for p in ("om", "op", "mp"):
        act_scalar(p)
    g.scalar.wait_ge(S.ypdone, 1)
    for i, (a, b, r) in enumerate(yout):
        g.scalar.activation(T.yout[:, a:b], T.yp[:, a:b], ActivationFunctionType.Copy).then_inc(S["ycopied%d" % i], 1)
    act_scalar("mm")

    act_vector("om")
    pack("om")
    act_vector("op")
    act_vector("mp")
    pack("op")
    pack("mp")
    act_vector("mm")
    pack("mm")
    g.vector.wait_ge(S.ymdone, 1)
    for i, (a, b, r) in enumerate(yin):
        g.vector.wait_ge(S["goty%d" % i], count(role[r], partner, ENGINES["y" if r == "d" else "carry"]))
        g.vector.tensor_tensor(T.ysum[:, a:b], T.ym[:, a:b], T.yland[:, a:b], AluOpType.add).then_inc(S["ysummed%d" % i], 1)

    for i, (a, b, r) in enumerate(yin):
        g.sync.wait_ge(S["ysummed%d" % i], 1)
        g.sync.dma_start(T.y[:, a:b], T.ysum[:, a:b]).then_inc(S.stored, 16)
    g.sync.wait_ge(S.stored, 16 * len(yin))

    g.wait_ge(S.sent, n_sent[0])
